import numpy as np
import ml_dtypes


def mxq(x, axis, fmt="e4m3"):
    dtype, down = {"e4m3": (ml_dtypes.float8_e4m3fn, 7), "e5m2": (ml_dtypes.float8_e5m2, 14)}[fmt]
    v = np.moveaxis(np.asarray(x, np.float32).astype(ml_dtypes.bfloat16).astype(np.float64), axis, -1)
    blocks = v.reshape(v.shape[:-1] + (-1, 32))
    amax = np.abs(blocks).max(-1, keepdims=True)
    byte = np.maximum(np.where(amax > 0, np.frexp(amax)[1] - 1 + 127, 0) - down, 1)
    scale = np.exp2(byte - 127.0)
    codes = (blocks / scale).astype(np.float32).astype(dtype).astype(np.float64)
    return np.moveaxis((codes * scale).reshape(v.shape), -1, axis)


WIDE = False


def mx_kscale(k):
    if not WIDE:
        return np.ones(k)
    levels = np.array([10, -10, 5, -5, 0])
    if k % 512:
        return np.exp2(np.random.permutation(np.resize(levels, k // 32))).repeat(32)
    a = np.empty((k // 512, 16))
    for p in range(k // 512):
        a[p, :8] = np.random.permutation(np.resize(levels, 8))
        for g in range(8):
            far = levels[np.abs(levels - a[p, g]) >= 10]
            a[p, g + 8] = far[np.random.randint(len(far))]
    return np.exp2(a.ravel()).repeat(32)


BF16 = ml_dtypes.bfloat16


def bf(x):
    return np.asarray(x, np.float32).astype(BF16)


def f64(x):
    return np.asarray(x).astype(np.float64)


E2M1 = np.array([0.0, 0.5, 1.0, 1.5, 2.0, 3.0, 4.0, 6.0, -0.0, -0.5, -1.0, -1.5, -2.0, -3.0, -4.0, -6.0])


def pack_weight(w, fmt):
    k, n = w.shape
    w = f64(bf(w)).reshape(k // 32, 32, n)
    amax = np.abs(w).max(1)
    if fmt == "e4m3":
        byte = np.frexp(amax)[1] - 1 + 127 - 7
    else:
        mant, ex = np.frexp(amax / 6.0)
        byte = np.where(mant > 0.5, ex, ex - 1) + 127
    byte = np.clip(np.where(amax > 0, byte, 1), 1, 254)
    scaled = (w * np.exp2(127.0 - byte)[:, None, :]).reshape(k, n).astype(np.float32)
    by_word = np.ascontiguousarray(scaled.reshape(k // 512, 128, 4, n).transpose(0, 1, 3, 2))
    if fmt == "e4m3":
        words = by_word.astype(ml_dtypes.float8_e4m3fn).view(np.uint8)
    else:
        c = by_word.astype(ml_dtypes.float4_e2m1fn).view(np.uint8) & 0xF
        words = c[..., 0::2] | (c[..., 1::2] << 4)
    return np.ascontiguousarray(words), np.ascontiguousarray(byte.astype(np.uint8).reshape(k // 512, 16, n))


def unpack_weight(words, scales, fmt):
    g, p, n, _ = words.shape
    if fmt == "e4m3":
        vals = np.ascontiguousarray(words).view(ml_dtypes.float8_e4m3fn).astype(np.float64)
    else:
        nib = np.empty((g, p, n, 4), np.uint8)
        nib[..., 0::2] = words & 0xF
        nib[..., 1::2] = words >> 4
        vals = E2M1[nib]
    vals = vals * np.repeat(np.exp2(scales.astype(np.float64) - 127.0), 8, axis=1)[..., None]
    return vals.transpose(0, 1, 3, 2).reshape(g * 512, n)
def pack4(w):
    words, scales = pack_weight(w, "e2m1")
    return words.reshape(words.shape[0], 128, -1), scales


def unpack4(words, scales):
    return unpack_weight(words.reshape(words.shape[0], 128, -1, 2), scales, "e2m1")


E4M3FN = np.array([(-1.0 if i & 128 else 1.0) * ((1.0 + (i & 7) / 8.0) * 2.0 ** (((i >> 3) & 15) - 7) if i & 120 else (i & 7) * 2.0 ** -9) for i in range(256)])


def e4m3fn_bytes(y):
    return np.clip(np.asarray(y, np.float64), -448.0, 448.0).astype(np.float32).astype(ml_dtypes.float8_e4m3fn).view(np.uint8)


def e4m3fn_values(b):
    return E4M3FN[b]


B, T, D, H, K = 2, 1024, 1024, 4, 256
E = H * K


def draw0():
    s = mx_kscale(D)
    u = mx_kscale(T)
    x = bf(np.random.standard_normal((B, T, D)) * s)
    wk_words, wk_scales = pack4(np.random.standard_normal((D, E)) / np.sqrt(D) / s[:, None])
    wv_words, wv_scales = pack4(np.random.standard_normal((D, E)) / np.sqrt(D) / s[:, None])
    return {
        "x": x,
        "wk_words": wk_words,
        "wk_scales": wk_scales,
        "wv_words": wv_words,
        "wv_scales": wv_scales,
        "dec": bf(np.random.uniform(0.3, 1.0, (B, T, H)) * u[None, :, None]),
        "beta": bf(np.random.uniform(0.5, 1.5, (B, T)) / u[None, :]),
        "gamma": bf(np.random.uniform(0.3, 0.9, (B, H))),
        "s_prev": bf(np.random.standard_normal((B, H, K, K))),
    }


def project_heads(xq, w, heads):
    b, t, _ = xq.shape
    e = w.shape[1]
    return (xq @ w).reshape(b, t, heads, e // heads)


def core(x, wk_words, wk_scales, wv_words, wv_scales, dec, beta, gamma, s_prev):
    t = x.shape[1]
    heads = dec.shape[2]
    xq = mxq(f64(x), 2, "e4m3")
    k = project_heads(xq, unpack4(wk_words, wk_scales), heads)
    v = project_heads(xq, unpack4(wv_words, wv_scales), heads)
    kd = k * f64(dec)[:, :, :, None]
    vb = v * f64(beta)[:, :, None, None]
    kdq = mxq(kd.transpose(0, 2, 3, 1), 3, "e4m3")
    vbq = mxq(vb.transpose(0, 2, 1, 3), 2, "e4m3")
    m = (kdq @ vbq) / np.sqrt(t)
    return f64(gamma)[:, :, None, None] * f64(s_prev) + m


def setup_inputs():
    drawn = draw0()
    full = np.asarray(drawn['x']).astype(np.float64)
    scale = (np.abs(full).reshape(2, 8, 128, 8, 128).max(axis=(2, 4)) / 448.0).astype(np.float32)
    given = {}
    for key, value in drawn.items():
        if key == 'x':
            given['x_bytes'] = e4m3fn_bytes(full / np.repeat(np.repeat(scale.astype(np.float64), 128, axis=1), 128, axis=2))
            given['x_scale'] = scale
        else:
            given[key] = value
    return given


def reference(x_bytes, x_scale, wk_words, wk_scales, wv_words, wv_scales, dec, beta, gamma, s_prev):
    return core(e4m3fn_values(x_bytes) * np.repeat(np.repeat(x_scale.astype(np.float64), 128, axis=1), 128, axis=2), wk_words, wk_scales, wv_words, wv_scales, dec, beta, gamma, s_prev)

@@ -1,0 +1,311 @@
+from contextlib import ExitStack
+
+import concourse.mybir as mybir
+from concourse.masks import make_identity
+
+B, T, D, H, K = 2, 1024, 1024, 4, 256
+E = H * K
+FLOPS = 2 * B * T * D * 2 * E + 2 * B * H * K * K * T
+
+F32 = mybir.dt.float32
+BF16 = mybir.dt.bfloat16
+I32 = mybir.dt.int32
+U32 = mybir.dt.uint32
+U8 = mybir.dt.uint8
+E4M3FN = mybir.dt.float8_e4m3fn
+E4M3X4 = mybir.dt.float8_e4m3fn_x4
+E2M1X4 = mybir.dt.float4_e2m1fn_x4
+MULT = mybir.AluOpType.mult
+ADD = mybir.AluOpType.add
+COPY = mybir.ActivationFunctionType.Copy
+
+P = 128
+GT = 512
+N_GROUPS = B * T // GT
+G = D // 512
+J = D // 128
+
+
+def tile_yocogatedretentionchunkstate_d2p_kernel(
+    tc, x_bytes, x_scale, wk_words, wk_scales, wv_words, wv_scales, dec, beta, gamma, s_prev, out
+):
+    nc = tc.nc
+    with ExitStack() as ctx:
+        keep = ctx.enter_context(tc.tile_pool(name="keep", bufs=1))
+        work = ctx.enter_context(tc.tile_pool(name="work", bufs=1))
+        ring = ctx.enter_context(tc.psum_pool(name="ring", bufs=6))
+        mixp = ctx.enter_context(tc.psum_pool(name="mixp", bufs=2))
+        ctx.enter_context(tc.manual_schedule())
+
+        xb = [keep.tile([P, 4, D], U8, name="xb%d" % n, align_bytes=64) for n in range(N_GROUPS)]
+        xs = keep.tile([P, N_GROUPS, J], F32, name="xs")
+        words = [keep.tile([P, G, 2 * E], U8, name="words%d" % i, align_bytes=64) for i in range(2)]
+        wsc = [keep.tile([P, G, E], U8, name="wsc%d" % i, align_bytes=64) for i in range(2)]
+        dec_bf = keep.tile([P, N_GROUPS, 4 * H], BF16, name="dec_bf")
+        beta_bf = keep.tile([P, N_GROUPS, 4], BF16, name="beta_bf")
+        gamma_bf = keep.tile([P, B * H], BF16, name="gamma_bf")
+        dec32 = keep.tile([P, N_GROUPS, 4 * H], F32, name="dec32")
+        beta_f = keep.tile([P, N_GROUPS, 4], F32, name="beta_f")
+        gamma_f = keep.tile([P, B * H], F32, name="gamma_f")
+        sp = [keep.tile([P, H * 2, K], BF16, name="sp%d" % b, align_bytes=64) for b in range(B)]
+        ident = keep.tile([P, P], F32, name="ident")
+        xq = [keep.tile([P, 4 * G * P], U32, name="xq%d" % n, align_bytes=64) for n in range(N_GROUPS)]
+        xqs = [keep.tile([P, 4 * G * P], U8, name="xqs%d" % n, align_bytes=64) for n in range(N_GROUPS)]
+        kvq = [[keep.tile([P, 512], U32, name="kvq%d_%d" % (n, c), align_bytes=64) for c in range(4)] for n in range(N_GROUPS)]
+        kvs = [[keep.tile([P, 512], U8, name="kvs%d_%d" % (n, c), align_bytes=64) for c in range(4)] for n in range(N_GROUPS)]
+
+        x_rows = x_bytes.rearrange("b (g p t) k -> (b g) p t k", p=P, t=4)
+        x_blocks = x_scale.rearrange("b (g q) j -> (b g) q j", q=4)
+        w_hbm = (wk_words, wv_words)
+        s_hbm = (wk_scales, wv_scales)
+
+        def load_words(i, pair):
+            cols = slice(1024 * pair, 1024 * (pair + 1))
+            nc.sync.dma_start(out=words[i][:, :, cols], in_=w_hbm[i].rearrange("g p c -> p g c")[:, :, cols])
+
+        def load_wscales(i):
+            for q in range(4):
+                src = s_hbm[i][:, 4 * q : 4 * q + 4, :].bitcast(I32).rearrange("g r n -> r g n")
+                nc.sync.dma_start(out=wsc[i][32 * q : 32 * q + 4, :, :].bitcast(I32), in_=src)
+
+        for i in range(2):
+            nc.vector.memset(wsc[i][:].rearrange("p g n -> p (g n)").bitcast(I32), 0)
+        make_identity(nc, ident[:])
+
+        for q in range(4):
+            nc.scalar.dma_start(out=xs[32 * q : 32 * (q + 1), :, :], in_=x_blocks[:, q, :].partition_broadcast(32))
+        nc.sync.dma_start(out=xb[0][:, 0:1, :], in_=x_rows[0][:, 0:1, :])
+        nc.sync.dma_start(out=xb[0][:, 1:4, :], in_=x_rows[0][:, 1:4, :])
+        load_wscales(0)
+        load_words(0, 0)
+        load_wscales(1)
+        load_words(1, 0)
+        load_words(0, 1)
+        load_words(1, 1)
+        for n in range(1, N_GROUPS):
+            nc.sync.dma_start(out=xb[n][:], in_=x_rows[n])
+        for b in range(B):
+            nc.sync.dma_start(out=sp[b][:], in_=s_prev[b].rearrange("h (i p) j -> p (h i) j", p=P))
+
+        nc.gpsimd.dma_start(out=dec_bf[:], in_=dec.rearrange("b (g p t) h -> (b g) p (t h)", p=P, t=4).rearrange("n p c -> p n c"))
+        nc.gpsimd.dma_start(out=beta_bf[:], in_=beta.rearrange("b (g p t) -> (b g) p t", p=P, t=4).rearrange("n p t -> p n t"))
+        nc.gpsimd.dma_start(out=gamma_bf[:], in_=gamma.rearrange("b h -> (b h)").partition_broadcast(P))
+        nc.gpsimd.tensor_scalar(out=dec32[:], in0=dec_bf[:], scalar1=1.0 / 32.0, scalar2=None, op0=MULT)
+        nc.gpsimd.tensor_copy(out=beta_f[:], in_=beta_bf[:])
+        nc.gpsimd.tensor_copy(out=gamma_f[:], in_=gamma_bf[:])
+
+        xw, xin, planes, grouped = {}, {}, {}, {}
+
+        def widen(n, t, on_scalar=()):
+            tile = work.tile([P, D], BF16, name="xw", tag="xw", bufs=16, align_bytes=64)
+            xw[n, t] = tile
+            for j in range(J):
+                cols = slice(128 * j, 128 * (j + 1))
+                src = xb[n][:, t, cols].bitcast(E4M3FN)
+                if j in on_scalar:
+                    nc.scalar.activation(out=tile[:, cols], in_=src, func=COPY, scale=xs[:, n, j : j + 1])
+                else:
+                    nc.vector.tensor_scalar(out=tile[:, cols], in0=src, scalar1=xs[:, n, j : j + 1], scalar2=None, op0=MULT)
+
+        def turn(n, t):
+            if t % 2 == 0:
+                xin[n, t // 2] = work.tile([P, 2, G, P, 4], BF16, name="xin", tag="xin", bufs=4, align_bytes=64)
+            bank = ring.tile([P, 512], F32, name="bank", tag="bank", bufs=6)
+            view = bank[:].rearrange("p (g u m) -> p g u m", g=G, u=2)
+            src = xw[n, t][:].bitcast(F32)
+            for g in range(G):
+                for u in range(2):
+                    nc.tensor.transpose(view[:, g, u, :], src[:, 256 * g + u : 256 * (g + 1) : 2], ident[:])
+            dst = xin[n, t // 2][:, t % 2].bitcast(F32)
+            nc.scalar.copy(out=dst, in_=view.rearrange("p g u m -> p g m u"))
+
+        def quant_x(n, t, count):
+            cols = slice(256 * t, 256 * (t + count))
+            src = xin[n, t // 2][:, t % 2 : t % 2 + count].rearrange("p t g m w -> p (t g m w)")
+            nc.vector.quantize_mx(out=xq[n][:, cols].bitcast(E4M3X4), scales=xqs[n][:, cols], in_=src)
+
+        def project(n, c, t):
+            i, pair = c % 2, c // 2
+            if t == 0:
+                planes[n, c] = work.tile([P, 4, 512], BF16, name="planes", tag="planes", bufs=7, align_bytes=64)
+            bank = ring.tile([P, 512], F32, name="bank", tag="bank", bufs=6)
+            for g in range(G):
+                rows = slice(256 * t + 128 * g, 256 * t + 128 * (g + 1))
+                nc.tensor.matmul_mx(
+                    out=bank[:],
+                    lhsT=xq[n][:, rows].bitcast(E4M3X4),
+                    lhsT_scale=xqs[n][:, rows],
+                    rhs=words[i][:, g, 1024 * pair : 1024 * (pair + 1)].bitcast(E2M1X4),
+                    rhs_scale=wsc[i][:, g, 512 * pair : 512 * (pair + 1)],
+                    start=(g == 0),
+                    stop=(g == G - 1),
+                )
+            dst = planes[n, c]
+            if i == 0:
+                for e in range(2):
+                    col = 4 * t + 2 * pair + e
+                    half = slice(256 * e, 256 * (e + 1))
+                    nc.scalar.activation(out=dst[:, t, half], in_=bank[:, half], func=COPY, scale=dec32[:, n, col : col + 1])
+            else:
+                nc.scalar.activation(out=dst[:, t, :], in_=bank[:], func=COPY, scale=beta_f[:, n, t : t + 1])
+
+        def interleave(n, c):
+            tile = work.tile([P, 2048], BF16, name="grouped", tag="grouped", bufs=4, align_bytes=64)
+            grouped[n, c] = tile
+            nc.vector.tensor_copy(
+                out=tile[:].rearrange("p (c i t) -> p c t i", i=4, t=4),
+                in_=planes[n, c][:].rearrange("p t (c i) -> p c t i", i=4),
+            )
+
+        def quant(n, c):
+            nc.vector.quantize_mx(out=kvq[n][c][:].bitcast(E4M3X4), scales=kvs[n][c][:], in_=grouped[n, c][:])
+
+        mixed = {}
+
+        def mix(b, h):
+            ck, off = 2 * (h // 2), 256 * (h % 2)
+            bank = mixp.tile([P, 512], F32, name="mixbank", tag="mixbank", bufs=2)
+            mixed[b, h] = bank
+            for i in range(2):
+                rows = slice(off + 128 * i, off + 128 * (i + 1))
+                for g in range(2):
+                    n = 2 * b + g
+                    nc.tensor.matmul_mx(
+                        out=bank[:, 256 * i : 256 * (i + 1)],
+                        lhsT=kvq[n][ck][:, rows].bitcast(E4M3X4),
+                        lhsT_scale=kvs[n][ck][:, rows],
+                        rhs=kvq[n][ck + 1][:, off : off + 256].bitcast(E4M3X4),
+                        rhs_scale=kvs[n][ck + 1][:, off : off + 256],
+                        start=(g == 0),
+                        stop=(g == 1),
+                    )
+
+        def finish(b, h):
+            res = work.tile([P, 2, K], F32, name="res", tag="res", bufs=4)
+            nc.vector.scalar_tensor_tensor(
+                out=res[:].rearrange("p i j -> p (i j)"),
+                in0=sp[b][:, 2 * h : 2 * h + 2, :].rearrange("p i j -> p (i j)"),
+                scalar=gamma_f[:, H * b + h : H * b + h + 1],
+                in1=mixed[b, h][:],
+                op0=MULT,
+                op1=ADD,
+            )
+            nc.sync.dma_start(out=out[b, h].rearrange("(i p) j -> p i j", p=P), in_=res[:])
+
+        upper = (4, 5, 6, 7)
+
+        widen(0, 0, upper)
+        widen(0, 1)
+        turn(0, 0)
+        widen(0, 2)
+        turn(0, 1)
+        quant_x(0, 0, 1)
+        widen(0, 3)
+        quant_x(0, 1, 1)
+        for c in range(4):
+            project(0, c, 0)
+        turn(0, 2)
+        turn(0, 3)
+        widen(1, 0)
+        widen(1, 1)
+        for c in range(4):
+            project(0, c, 1)
+        quant_x(0, 2, 1)
+        quant_x(0, 3, 1)
+        widen(1, 2)
+        widen(1, 3, upper)
+        turn(1, 0)
+        turn(1, 1)
+        for c in range(4):
+            project(0, c, 2)
+        widen(2, 0)
+        quant_x(1, 0, 2)
+        widen(2, 1)
+        turn(1, 2)
+        turn(1, 3)
+        for c in range(4):
+            project(0, c, 3)
+        widen(2, 2)
+        widen(2, 3, upper)
+        quant_x(1, 2, 2)
+        for t in range(4):
+            widen(3, t, upper if t == 3 else ())
+
+        def project_all(n, c):
+            for t in range(4):
+                project(n, c, t)
+
+        interleave(0, 0)
+        project_all(1, 0)
+        turn(2, 0)
+        turn(2, 1)
+        interleave(0, 1)
+        quant(0, 0)
+        project_all(1, 1)
+        interleave(0, 2)
+        quant(0, 1)
+        quant_x(2, 0, 2)
+        project_all(1, 2)
+        turn(2, 2)
+        turn(2, 3)
+        interleave(0, 3)
+        quant(0, 2)
+        project_all(1, 3)
+        interleave(1, 0)
+        quant(0, 3)
+        quant_x(2, 2, 2)
+
+        project_all(2, 0)
+        turn(3, 0)
+        turn(3, 1)
+        interleave(1, 1)
+        quant(1, 0)
+        project_all(2, 1)
+        interleave(1, 2)
+        quant(1, 1)
+        quant_x(3, 0, 2)
+        mix(0, 0)
+        mix(0, 1)
+        project_all(2, 2)
+        turn(3, 2)
+        turn(3, 3)
+        interleave(1, 3)
+        quant(1, 2)
+        finish(0, 0)
+        finish(0, 1)
+        project_all(2, 3)
+        interleave(2, 0)
+        quant(1, 3)
+        quant_x(3, 2, 2)
+        mix(0, 2)
+        mix(0, 3)
+
+        project_all(3, 0)
+        interleave(2, 1)
+        quant(2, 0)
+        finish(0, 2)
+        finish(0, 3)
+        project_all(3, 1)
+        interleave(2, 2)
+        quant(2, 1)
+        project_all(3, 2)
+        interleave(2, 3)
+        quant(2, 2)
+        interleave(3, 0)
+        quant(2, 3)
+        project_all(3, 3)
+        interleave(3, 1)
+        quant(3, 0)
+        interleave(3, 2)
+        quant(3, 1)
+        mix(1, 0)
+        mix(1, 1)
+        interleave(3, 3)
+        quant(3, 2)
+        finish(1, 0)
+        quant(3, 3)
+        finish(1, 1)
+        mix(1, 2)
+        mix(1, 3)
+        finish(1, 2)
+        finish(1, 3)

@@ -63,32 +63,34 @@ def tile_yocogatedretentionchunkstate_d2p_kernel(
             cols = slice(1024 * pair, 1024 * (pair + 1))
             nc.sync.dma_start(out=words[i][:, :, cols], in_=w_hbm[i].rearrange("g p c -> p g c")[:, :, cols])
 
-        def load_wscales(i):
+        def load_wscales(i, queue):
             for q in range(4):
                 src = s_hbm[i][:, 4 * q : 4 * q + 4, :].bitcast(I32).rearrange("g r n -> r g n")
-                nc.sync.dma_start(out=wsc[i][32 * q : 32 * q + 4, :, :].bitcast(I32), in_=src)
+                queue.dma_start(out=wsc[i][32 * q : 32 * q + 4, :, :].bitcast(I32), in_=src)
 
         for i in range(2):
             nc.vector.memset(wsc[i][:].rearrange("p g n -> p (g n)").bitcast(I32), 0)
+
+        nc.gpsimd.dma_start(out=dec_bf[:], in_=dec.rearrange("b (g p t) h -> (b g) p (t h)", p=P, t=4).rearrange("n p c -> p n c"))
+        nc.gpsimd.dma_start(out=beta_bf[:], in_=beta.rearrange("b (g p t) -> (b g) p t", p=P, t=4).rearrange("n p t -> p n t"))
         make_identity(nc, ident[:])
 
         for q in range(4):
             nc.scalar.dma_start(out=xs[32 * q : 32 * (q + 1), :, :], in_=x_blocks[:, q, :].partition_broadcast(32))
         nc.sync.dma_start(out=xb[0][:, 0:1, :], in_=x_rows[0][:, 0:1, :])
         nc.sync.dma_start(out=xb[0][:, 1:4, :], in_=x_rows[0][:, 1:4, :])
-        load_wscales(0)
         load_words(0, 0)
-        load_wscales(1)
+        load_wscales(0, nc.sync)
+        load_wscales(1, nc.gpsimd)
+        nc.sync.dma_start(out=xb[1][:], in_=x_rows[1])
         load_words(1, 0)
         load_words(0, 1)
         load_words(1, 1)
-        for n in range(1, N_GROUPS):
+        for n in range(2, N_GROUPS):
             nc.sync.dma_start(out=xb[n][:], in_=x_rows[n])
         for b in range(B):
             nc.sync.dma_start(out=sp[b][:], in_=s_prev[b].rearrange("h (i p) j -> p (h i) j", p=P))
 
-        nc.gpsimd.dma_start(out=dec_bf[:], in_=dec.rearrange("b (g p t) h -> (b g) p (t h)", p=P, t=4).rearrange("n p c -> p n c"))
-        nc.gpsimd.dma_start(out=beta_bf[:], in_=beta.rearrange("b (g p t) -> (b g) p t", p=P, t=4).rearrange("n p t -> p n t"))
         nc.gpsimd.dma_start(out=gamma_bf[:], in_=gamma.rearrange("b h -> (b h)").partition_broadcast(P))
         nc.gpsimd.tensor_scalar(out=dec32[:], in0=dec_bf[:], scalar1=1.0 / 32.0, scalar2=None, op0=MULT)
         nc.gpsimd.tensor_copy(out=beta_f[:], in_=beta_bf[:])
@@ -96,16 +98,15 @@ def tile_yocogatedretentionchunkstate_d2p_kernel(
 
         xw, xin, planes, grouped = {}, {}, {}, {}
 
-        def widen(n, t, on_scalar=()):
+        def widen(n, t):
             tile = work.tile([P, D], BF16, name="xw", tag="xw", bufs=16, align_bytes=64)
             xw[n, t] = tile
+            dst = tile[:].rearrange("p (g u m e) -> p g m u e", g=G, u=2, e=2)
             for j in range(J):
-                cols = slice(128 * j, 128 * (j + 1))
-                src = xb[n][:, t, cols].bitcast(E4M3FN)
-                if j in on_scalar:
-                    nc.scalar.activation(out=tile[:, cols], in_=src, func=COPY, scale=xs[:, n, j : j + 1])
-                else:
-                    nc.vector.tensor_scalar(out=tile[:, cols], in0=src, scalar1=xs[:, n, j : j + 1], scalar2=None, op0=MULT)
+                src = xb[n][:, t, 128 * j : 128 * (j + 1)].bitcast(E4M3FN).rearrange("p (m u e) -> p m u e", u=2, e=2)
+                nc.vector.tensor_scalar(
+                    out=dst[:, j // 4, 32 * (j % 4) : 32 * (j % 4 + 1)], in0=src, scalar1=xs[:, n, j : j + 1], scalar2=None, op0=MULT
+                )
 
         def turn(n, t):
             if t % 2 == 0:
@@ -115,7 +116,7 @@ def tile_yocogatedretentionchunkstate_d2p_kernel(
             src = xw[n, t][:].bitcast(F32)
             for g in range(G):
                 for u in range(2):
-                    nc.tensor.transpose(view[:, g, u, :], src[:, 256 * g + u : 256 * (g + 1) : 2], ident[:])
+                    nc.tensor.transpose(view[:, g, u, :], src[:, 256 * g + 128 * u : 256 * g + 128 * (u + 1)], ident[:])
             dst = xin[n, t // 2][:, t % 2].bitcast(F32)
             nc.scalar.copy(out=dst, in_=view.rearrange("p g u m -> p g m u"))
 
@@ -149,16 +150,19 @@ def tile_yocogatedretentionchunkstate_d2p_kernel(
             else:
                 nc.scalar.activation(out=dst[:, t, :], in_=bank[:], func=COPY, scale=beta_f[:, n, t : t + 1])
 
-        def interleave(n, c):
-            tile = work.tile([P, 2048], BF16, name="grouped", tag="grouped", bufs=4, align_bytes=64)
-            grouped[n, c] = tile
-            nc.vector.tensor_copy(
-                out=tile[:].rearrange("p (c i t) -> p c t i", i=4, t=4),
-                in_=planes[n, c][:].rearrange("p t (c i) -> p c t i", i=4),
+        def interleave(n, c, half=None, copy=nc.vector.tensor_copy):
+            if (n, c) not in grouped:
+                grouped[n, c] = work.tile([P, 2048], BF16, name="grouped", tag="grouped", bufs=4, align_bytes=64)
+            cols = slice(0, 512) if half is None else slice(256 * half, 256 * (half + 1))
+            copy(
+                out=grouped[n, c][:].rearrange("p (c t) -> p c t", t=4)[:, cols, :].rearrange("p (c i) t -> p c t i", i=4),
+                in_=planes[n, c][:, :, cols].rearrange("p t (c i) -> p c t i", i=4),
             )
 
-        def quant(n, c):
-            nc.vector.quantize_mx(out=kvq[n][c][:].bitcast(E4M3X4), scales=kvs[n][c][:], in_=grouped[n, c][:])
+        def quant(n, c, half=None):
+            cols = slice(0, 512) if half is None else slice(256 * half, 256 * (half + 1))
+            wide = slice(4 * cols.start, 4 * cols.stop)
+            nc.vector.quantize_mx(out=kvq[n][c][:, cols].bitcast(E4M3X4), scales=kvs[n][c][:, cols], in_=grouped[n, c][:, wide])
 
         mixed = {}
 
@@ -180,132 +184,83 @@ def tile_yocogatedretentionchunkstate_d2p_kernel(
                         stop=(g == 1),
                     )
 
-        def finish(b, h):
-            res = work.tile([P, 2, K], F32, name="res", tag="res", bufs=4)
-            nc.vector.scalar_tensor_tensor(
-                out=res[:].rearrange("p i j -> p (i j)"),
-                in0=sp[b][:, 2 * h : 2 * h + 2, :].rearrange("p i j -> p (i j)"),
-                scalar=gamma_f[:, H * b + h : H * b + h + 1],
-                in1=mixed[b, h][:],
-                op0=MULT,
-                op1=ADD,
-            )
-            nc.sync.dma_start(out=out[b, h].rearrange("(i p) j -> p i j", p=P), in_=res[:])
-
-        upper = (4, 5, 6, 7)
-
-        widen(0, 0, upper)
-        widen(0, 1)
-        turn(0, 0)
-        widen(0, 2)
-        turn(0, 1)
-        quant_x(0, 0, 1)
-        widen(0, 3)
-        quant_x(0, 1, 1)
-        for c in range(4):
-            project(0, c, 0)
-        turn(0, 2)
-        turn(0, 3)
-        widen(1, 0)
-        widen(1, 1)
-        for c in range(4):
-            project(0, c, 1)
-        quant_x(0, 2, 1)
-        quant_x(0, 3, 1)
-        widen(1, 2)
-        widen(1, 3, upper)
-        turn(1, 0)
-        turn(1, 1)
-        for c in range(4):
-            project(0, c, 2)
-        widen(2, 0)
-        quant_x(1, 0, 2)
-        widen(2, 1)
-        turn(1, 2)
-        turn(1, 3)
-        for c in range(4):
-            project(0, c, 3)
-        widen(2, 2)
-        widen(2, 3, upper)
-        quant_x(1, 2, 2)
-        for t in range(4):
-            widen(3, t, upper if t == 3 else ())
+        def finish(b, h, parts=1):
+            res = work.tile([P, 512], F32, name="res", tag="res", bufs=4)
+            state = sp[b][:, 2 * h : 2 * h + 2, :].rearrange("p i j -> p (i j)")
+            width = 512 // parts
+            for i in range(parts):
+                cols = slice(width * i, width * (i + 1))
+                nc.vector.scalar_tensor_tensor(
+                    out=res[:, cols],
+                    in0=state[:, cols],
+                    scalar=gamma_f[:, H * b + h : H * b + h + 1],
+                    in1=mixed[b, h][:, cols],
+                    op0=MULT,
+                    op1=ADD,
+                )
+                rows = out[b, h].rearrange("(i p) j -> p i j", p=P)
+                each = 2 // parts
+                nc.sync.dma_start(out=rows[:, each * i : each * (i + 1), :], in_=res[:, cols].rearrange("p (i j) -> p i j", j=K))
 
         def project_all(n, c):
             for t in range(4):
                 project(n, c, t)
 
-        interleave(0, 0)
-        project_all(1, 0)
-        turn(2, 0)
-        turn(2, 1)
-        interleave(0, 1)
-        quant(0, 0)
-        project_all(1, 1)
-        interleave(0, 2)
-        quant(0, 1)
-        quant_x(2, 0, 2)
-        project_all(1, 2)
-        turn(2, 2)
-        turn(2, 3)
-        interleave(0, 3)
-        quant(0, 2)
-        project_all(1, 3)
-        interleave(1, 0)
-        quant(0, 3)
-        quant_x(2, 2, 2)
+        for t in range(3):
+            widen(0, t)
+        turn(0, 0)
+        quant_x(0, 0, 1)
+        widen(0, 3)
+        turn(0, 1)
+        quant_x(0, 1, 1)
+        widen(1, 0)
+        turn(0, 2)
+        quant_x(0, 2, 1)
+        widen(1, 1)
+        turn(0, 3)
+        quant_x(0, 3, 1)
+        for n, t in ((1, 2), (1, 3), (2, 0), (2, 1)):
+            widen(n, t)
 
-        project_all(2, 0)
-        turn(3, 0)
-        turn(3, 1)
-        interleave(1, 1)
-        quant(1, 0)
-        project_all(2, 1)
-        interleave(1, 2)
-        quant(1, 1)
-        quant_x(3, 0, 2)
-        mix(0, 0)
-        mix(0, 1)
-        project_all(2, 2)
-        turn(3, 2)
-        turn(3, 3)
-        interleave(1, 3)
-        quant(1, 2)
-        finish(0, 0)
-        finish(0, 1)
-        project_all(2, 3)
-        interleave(2, 0)
-        quant(1, 3)
-        quant_x(3, 2, 2)
-        mix(0, 2)
-        mix(0, 3)
+        fill = {}
+        fill[0, 2] = [(widen, (2, 2)), (widen, (2, 3))]
+        fill[0, 3] = [(widen, (3, 0)), (widen, (3, 1))]
+        fill[1, 2] = [(widen, (3, 2))]
+        fill[1, 3] = [(widen, (3, 3))]
+        fill[2, 2] = [(finish, (0, 0)), (finish, (0, 1))]
+        fill[3, 0] = [(finish, (0, 2)), (finish, (0, 3))]
+        for n in range(N_GROUPS - 1):
+            fill[n, 0] = [(quant_x, (n + 1, 0, 2))]
+            fill[n, 1] = [(quant_x, (n + 1, 2, 2))]
+        heads = {(2, 1): (0, 0), (3, 0): (0, 2), (3, 3): (1, 0)}
 
-        project_all(3, 0)
-        interleave(2, 1)
-        quant(2, 0)
-        finish(0, 2)
-        finish(0, 3)
-        project_all(3, 1)
-        interleave(2, 2)
-        quant(2, 1)
-        project_all(3, 2)
-        interleave(2, 3)
-        quant(2, 2)
-        interleave(3, 0)
-        quant(2, 3)
-        project_all(3, 3)
-        interleave(3, 1)
-        quant(3, 0)
-        interleave(3, 2)
-        quant(3, 1)
-        mix(1, 0)
-        mix(1, 1)
-        interleave(3, 3)
-        quant(3, 2)
-        finish(1, 0)
-        quant(3, 3)
-        finish(1, 1)
+        for n in range(N_GROUPS):
+            for c in range(4):
+                project_all(n, c)
+                if n + 1 < N_GROUPS and c < 2:
+                    turn(n + 1, 2 * c)
+                    turn(n + 1, 2 * c + 1)
+                if (n, c) in heads:
+                    b, h = heads[n, c]
+                    mix(b, h)
+                    mix(b, h + 1)
+                if (n, c) == (3, 3):
+                    finish(1, 0)
+                    finish(1, 1)
+                if (n, c) in fill:
+                    interleave(n, c)
+                    for step, args in fill[n, c]:
+                        step(*args)
+                    quant(n, c)
+                else:
+                    interleave(n, c, 0)
+                    if (n, c) == (3, 3):
+                        interleave(n, c, 1, nc.scalar.copy)
+                    else:
+                        interleave(n, c, 1)
+                    quant(n, c, 0)
+                    quant(n, c, 1)
         mix(1, 2)
         mix(1, 3)
         finish(1, 2)
-        finish(1, 3)
+        finish(1, 3, 2)

@@ -46,7 +46,6 @@ def tile_yocogatedretentionchunkstate_d2p_kernel(
         gamma_bf = keep.tile([P, B * H], BF16, name="gamma_bf")
         dec32 = keep.tile([P, N_GROUPS, 4 * H], F32, name="dec32")
         beta_f = keep.tile([P, N_GROUPS, 4], F32, name="beta_f")
-        gamma_f = keep.tile([P, B * H], F32, name="gamma_f")
         sp = [keep.tile([P, H * 2, K], BF16, name="sp%d" % b, align_bytes=64) for b in range(B)]
         ident = keep.tile([P, P], F32, name="ident")
         xq = [keep.tile([P, 4 * G * P], U32, name="xq%d" % n, align_bytes=64) for n in range(N_GROUPS)]
@@ -71,8 +70,6 @@ def tile_yocogatedretentionchunkstate_d2p_kernel(
         for i in range(2):
             nc.vector.memset(wsc[i][:].rearrange("p g n -> p (g n)").bitcast(I32), 0)
 
-        nc.gpsimd.dma_start(out=dec_bf[:], in_=dec.rearrange("b (g p t) h -> (b g) p (t h)", p=P, t=4).rearrange("n p c -> p n c"))
-        nc.gpsimd.dma_start(out=beta_bf[:], in_=beta.rearrange("b (g p t) -> (b g) p t", p=P, t=4).rearrange("n p t -> p n t"))
         make_identity(nc, ident[:])
 
         for q in range(4):
@@ -81,31 +78,28 @@ def tile_yocogatedretentionchunkstate_d2p_kernel(
         nc.sync.dma_start(out=xb[0][:, 1:4, :], in_=x_rows[0][:, 1:4, :])
         load_words(0, 0)
         load_wscales(0, nc.sync)
-        load_wscales(1, nc.gpsimd)
+        nc.sync.dma_start(out=dec_bf[:], in_=dec.rearrange("b (g p t) h -> (b g) p (t h)", p=P, t=4).rearrange("n p c -> p n c"))
         nc.sync.dma_start(out=xb[1][:], in_=x_rows[1])
+        load_wscales(1, nc.sync)
+        nc.sync.dma_start(out=beta_bf[:], in_=beta.rearrange("b (g p t) -> (b g) p t", p=P, t=4).rearrange("n p t -> p n t"))
         load_words(1, 0)
         load_words(0, 1)
         load_words(1, 1)
         for n in range(2, N_GROUPS):
             nc.sync.dma_start(out=xb[n][:], in_=x_rows[n])
+        nc.sync.dma_start(out=gamma_bf[:], in_=gamma.rearrange("b h -> (b h)").partition_broadcast(P))
         for b in range(B):
             nc.sync.dma_start(out=sp[b][:], in_=s_prev[b].rearrange("h (i p) j -> p (h i) j", p=P))
-
-        nc.gpsimd.dma_start(out=gamma_bf[:], in_=gamma.rearrange("b h -> (b h)").partition_broadcast(P))
-        nc.gpsimd.tensor_scalar(out=dec32[:], in0=dec_bf[:], scalar1=1.0 / 32.0, scalar2=None, op0=MULT)
-        nc.gpsimd.tensor_copy(out=beta_f[:], in_=beta_bf[:])
-        nc.gpsimd.tensor_copy(out=gamma_f[:], in_=gamma_bf[:])
 
         xw, xin, planes, grouped = {}, {}, {}, {}
 
         def widen(n, t):
             tile = work.tile([P, D], BF16, name="xw", tag="xw", bufs=16, align_bytes=64)
             xw[n, t] = tile
-            dst = tile[:].rearrange("p (g u m e) -> p g m u e", g=G, u=2, e=2)
             for j in range(J):
-                src = xb[n][:, t, 128 * j : 128 * (j + 1)].bitcast(E4M3FN).rearrange("p (m u e) -> p m u e", u=2, e=2)
+                cols = slice(128 * j, 128 * (j + 1))
                 nc.vector.tensor_scalar(
-                    out=dst[:, j // 4, 32 * (j % 4) : 32 * (j % 4 + 1)], in0=src, scalar1=xs[:, n, j : j + 1], scalar2=None, op0=MULT
+                    out=tile[:, cols], in0=xb[n][:, t, cols].bitcast(E4M3FN), scalar1=xs[:, n, j : j + 1], scalar2=None, op0=MULT
                 )
 
         def turn(n, t):
@@ -116,7 +110,7 @@ def tile_yocogatedretentionchunkstate_d2p_kernel(
             src = xw[n, t][:].bitcast(F32)
             for g in range(G):
                 for u in range(2):
-                    nc.tensor.transpose(view[:, g, u, :], src[:, 256 * g + 128 * u : 256 * g + 128 * (u + 1)], ident[:])
+                    nc.tensor.transpose(view[:, g, u, :], src[:, 256 * g + u : 256 * (g + 1) : 2], ident[:])
             dst = xin[n, t // 2][:, t % 2].bitcast(F32)
             nc.scalar.copy(out=dst, in_=view.rearrange("p g u m -> p g m u"))
 
@@ -193,7 +187,7 @@ def tile_yocogatedretentionchunkstate_d2p_kernel(
                 nc.vector.scalar_tensor_tensor(
                     out=res[:, cols],
                     in0=state[:, cols],
-                    scalar=gamma_f[:, H * b + h : H * b + h + 1],
+                    scalar=gamma_bf[:, H * b + h : H * b + h + 1],
                     in1=mixed[b, h][:, cols],
                     op0=MULT,
                     op1=ADD,
@@ -236,6 +230,10 @@ def tile_yocogatedretentionchunkstate_d2p_kernel(
 
         for n in range(N_GROUPS):
             for c in range(4):
+                if (n, c) == (0, 0):
+                    nc.scalar.activation(out=dec32[:], in_=dec_bf[:], func=COPY, scale=1.0 / 32.0)
+                if (n, c) == (0, 1):
+                    nc.scalar.copy(out=beta_f[:], in_=beta_bf[:])
                 project_all(n, c)
                 if n + 1 < N_GROUPS and c < 2:
                     turn(n + 1, 2 * c)

@@ -93,14 +93,17 @@ def tile_yocogatedretentionchunkstate_d2p_kernel(
 
         xw, xin, planes, grouped = {}, {}, {}, {}
 
-        def widen(n, t):
-            tile = work.tile([P, D], BF16, name="xw", tag="xw", bufs=16, align_bytes=64)
-            xw[n, t] = tile
-            for j in range(J):
-                cols = slice(128 * j, 128 * (j + 1))
-                nc.vector.tensor_scalar(
-                    out=tile[:, cols], in0=xb[n][:, t, cols].bitcast(E4M3FN), scalar1=xs[:, n, j : j + 1], scalar2=None, op0=MULT
-                )
+        def widen(n, t, blocks=range(J), on_scalar=False):
+            if (n, t) not in xw:
+                xw[n, t] = work.tile([P, D], BF16, name="xw", tag="xw", bufs=16, align_bytes=64)
+            for j in blocks:
+                dst = xw[n, t][:, 128 * j : 128 * (j + 1)]
+                src = xb[n][:, t, 128 * j : 128 * (j + 1)].bitcast(E4M3FN)
+                scale = xs[:, n, j : j + 1]
+                if on_scalar:
+                    nc.scalar.activation(out=dst, in_=src, func=COPY, scale=scale)
+                else:
+                    nc.vector.tensor_scalar(out=dst, in0=src, scalar1=scale, scalar2=None, op0=MULT)
 
         def turn(n, t):
             if t % 2 == 0:
@@ -144,19 +147,20 @@ def tile_yocogatedretentionchunkstate_d2p_kernel(
             else:
                 nc.scalar.activation(out=dst[:, t, :], in_=bank[:], func=COPY, scale=beta_f[:, n, t : t + 1])
 
-        def interleave(n, c, half=None, copy=nc.vector.tensor_copy):
+        def interleave(n, c, first=0, last=512, copy=nc.vector.tensor_copy):
             if (n, c) not in grouped:
                 grouped[n, c] = work.tile([P, 2048], BF16, name="grouped", tag="grouped", bufs=4, align_bytes=64)
-            cols = slice(0, 512) if half is None else slice(256 * half, 256 * (half + 1))
             copy(
-                out=grouped[n, c][:].rearrange("p (c t) -> p c t", t=4)[:, cols, :].rearrange("p (c i) t -> p c t i", i=4),
-                in_=planes[n, c][:, :, cols].rearrange("p t (c i) -> p c t i", i=4),
+                out=grouped[n, c][:, 4 * first : 4 * last].rearrange("p (c i t) -> p c t i", i=4, t=4),
+                in_=planes[n, c][:, :, first:last].rearrange("p t (c i) -> p c t i", i=4),
             )
 
-        def quant(n, c, half=None):
-            cols = slice(0, 512) if half is None else slice(256 * half, 256 * (half + 1))
-            wide = slice(4 * cols.start, 4 * cols.stop)
-            nc.vector.quantize_mx(out=kvq[n][c][:, cols].bitcast(E4M3X4), scales=kvs[n][c][:, cols], in_=grouped[n, c][:, wide])
+        def quant(n, c, first=0, last=512):
+            nc.vector.quantize_mx(
+                out=kvq[n][c][:, first:last].bitcast(E4M3X4),
+                scales=kvs[n][c][:, first:last],
+                in_=grouped[n, c][:, 4 * first : 4 * last],
+            )
 
         mixed = {}
 
@@ -200,11 +204,13 @@ def tile_yocogatedretentionchunkstate_d2p_kernel(
             for t in range(4):
                 project(n, c, t)
 
-        for t in range(3):
-            widen(0, t)
+        widen(0, 0)
+        widen(0, 1)
+        widen(0, 2)
+        widen(0, 3, range(4), on_scalar=True)
         turn(0, 0)
         quant_x(0, 0, 1)
-        widen(0, 3)
+        widen(0, 3, range(4, J))
         turn(0, 1)
         quant_x(0, 1, 1)
         widen(1, 0)
@@ -215,6 +221,7 @@ def tile_yocogatedretentionchunkstate_d2p_kernel(
         quant_x(0, 3, 1)
         for n, t in ((1, 2), (1, 3), (2, 0), (2, 1)):
             widen(n, t)
+        nc.scalar.activation(out=dec32[:], in_=dec_bf[:], func=COPY, scale=1.0 / 32.0)
 
         fill = {}
         fill[0, 2] = [(widen, (2, 2)), (widen, (2, 3))]
@@ -224,20 +231,17 @@ def tile_yocogatedretentionchunkstate_d2p_kernel(
         fill[2, 2] = [(finish, (0, 0)), (finish, (0, 1))]
         fill[3, 0] = [(finish, (0, 2)), (finish, (0, 3))]
         for n in range(N_GROUPS - 1):
-            fill[n, 0] = [(quant_x, (n + 1, 0, 2))]
-            fill[n, 1] = [(quant_x, (n + 1, 2, 2))]
-        heads = {(2, 1): (0, 0), (3, 0): (0, 2), (3, 3): (1, 0)}
+            fill[n, 1] = [(quant_x, (n + 1, 0, 2)), (quant_x, (n + 1, 2, 2))]
+        heads = {(2, 2): (0, 0), (3, 0): (0, 2), (3, 3): (1, 0)}
 
         for n in range(N_GROUPS):
             for c in range(4):
-                if (n, c) == (0, 0):
-                    nc.scalar.activation(out=dec32[:], in_=dec_bf[:], func=COPY, scale=1.0 / 32.0)
                 if (n, c) == (0, 1):
                     nc.scalar.copy(out=beta_f[:], in_=beta_bf[:])
                 project_all(n, c)
-                if n + 1 < N_GROUPS and c < 2:
-                    turn(n + 1, 2 * c)
-                    turn(n + 1, 2 * c + 1)
+                if n + 1 < N_GROUPS and c == 1:
+                    for t in range(4):
+                        turn(n + 1, t)
                 if (n, c) in heads:
                     b, h = heads[n, c]
                     mix(b, h)
@@ -245,19 +249,21 @@ def tile_yocogatedretentionchunkstate_d2p_kernel(
                 if (n, c) == (3, 3):
                     finish(1, 0)
                     finish(1, 1)
-                if (n, c) in fill:
+                    interleave(n, c, 0, 256)
+                    interleave(n, c, 384, 512, nc.scalar.copy)
+                    interleave(n, c, 256, 384)
+                    quant(n, c, 0, 256)
+                    quant(n, c, 256, 512)
+                elif (n, c) in fill:
                     interleave(n, c)
                     for step, args in fill[n, c]:
                         step(*args)
                     quant(n, c)
                 else:
-                    interleave(n, c, 0)
-                    if (n, c) == (3, 3):
-                        interleave(n, c, 1, nc.scalar.copy)
-                    else:
-                        interleave(n, c, 1)
-                    quant(n, c, 0)
-                    quant(n, c, 1)
+                    interleave(n, c, 0, 256)
+                    interleave(n, c, 256, 512)
+                    quant(n, c, 0, 256)
+                    quant(n, c, 256, 512)
         mix(1, 2)
         mix(1, 3)
         finish(1, 2)

from contextlib import ExitStack

import concourse.mybir as mybir
from concourse.masks import make_identity

B, T, D, H, K = 2, 1024, 1024, 4, 256
E = H * K
FLOPS = 2 * B * T * D * 2 * E + 2 * B * H * K * K * T

F32 = mybir.dt.float32
BF16 = mybir.dt.bfloat16
I32 = mybir.dt.int32
U32 = mybir.dt.uint32
U8 = mybir.dt.uint8
E4M3FN = mybir.dt.float8_e4m3fn
E4M3X4 = mybir.dt.float8_e4m3fn_x4
E2M1X4 = mybir.dt.float4_e2m1fn_x4
MULT = mybir.AluOpType.mult
ADD = mybir.AluOpType.add
COPY = mybir.ActivationFunctionType.Copy

P = 128
GT = 512
N_GROUPS = B * T // GT
G = D // 512
J = D // 128


def tile_yocogatedretentionchunkstate_d2p_kernel(
    tc, x_bytes, x_scale, wk_words, wk_scales, wv_words, wv_scales, dec, beta, gamma, s_prev, out
):
    nc = tc.nc
    with ExitStack() as ctx:
        keep = ctx.enter_context(tc.tile_pool(name="keep", bufs=1))
        work = ctx.enter_context(tc.tile_pool(name="work", bufs=1))
        ring = ctx.enter_context(tc.psum_pool(name="ring", bufs=6))
        mixp = ctx.enter_context(tc.psum_pool(name="mixp", bufs=2))
        ctx.enter_context(tc.manual_schedule())

        xb = [keep.tile([P, 4, D], U8, name="xb%d" % n, align_bytes=64) for n in range(N_GROUPS)]
        xs = keep.tile([P, N_GROUPS, J], F32, name="xs")
        words = [keep.tile([P, G, 2 * E], U8, name="words%d" % i, align_bytes=64) for i in range(2)]
        wsc = [keep.tile([P, G, E], U8, name="wsc%d" % i, align_bytes=64) for i in range(2)]
        dec_bf = keep.tile([P, N_GROUPS, 4 * H], BF16, name="dec_bf")
        beta_bf = keep.tile([P, N_GROUPS, 4], BF16, name="beta_bf")
        gamma_bf = keep.tile([P, B * H], BF16, name="gamma_bf")
        dec32 = keep.tile([P, N_GROUPS, 4 * H], F32, name="dec32")
        beta_f = keep.tile([P, N_GROUPS, 4], F32, name="beta_f")
        sp = [keep.tile([P, H * 2, K], BF16, name="sp%d" % b, align_bytes=64) for b in range(B)]
        ident = keep.tile([P, P], F32, name="ident")
        xq = [keep.tile([P, 4 * G * P], U32, name="xq%d" % n, align_bytes=64) for n in range(N_GROUPS)]
        xqs = [keep.tile([P, 4 * G * P], U8, name="xqs%d" % n, align_bytes=64) for n in range(N_GROUPS)]
        kvq = [[keep.tile([P, 512], U32, name="kvq%d_%d" % (n, c), align_bytes=64) for c in range(4)] for n in range(N_GROUPS)]
        kvs = [[keep.tile([P, 512], U8, name="kvs%d_%d" % (n, c), align_bytes=64) for c in range(4)] for n in range(N_GROUPS)]

        x_rows = x_bytes.rearrange("b (g p t) k -> (b g) p t k", p=P, t=4)
        x_blocks = x_scale.rearrange("b (g q) j -> (b g) q j", q=4)
        w_hbm = (wk_words, wv_words)
        s_hbm = (wk_scales, wv_scales)

        def load_words(i, pair):
            cols = slice(1024 * pair, 1024 * (pair + 1))
            nc.sync.dma_start(out=words[i][:, :, cols], in_=w_hbm[i].rearrange("g p c -> p g c")[:, :, cols])

        def load_wscales(i, queue):
            for q in range(4):
                src = s_hbm[i][:, 4 * q : 4 * q + 4, :].bitcast(I32).rearrange("g r n -> r g n")
                queue.dma_start(out=wsc[i][32 * q : 32 * q + 4, :, :].bitcast(I32), in_=src)

        for i in range(2):
            nc.vector.memset(wsc[i][:].rearrange("p g n -> p (g n)").bitcast(I32), 0)

        make_identity(nc, ident[:])

        for q in range(4):
            nc.scalar.dma_start(out=xs[32 * q : 32 * (q + 1), :, :], in_=x_blocks[:, q, :].partition_broadcast(32))
        nc.sync.dma_start(out=xb[0][:, 0:1, :], in_=x_rows[0][:, 0:1, :])
        nc.sync.dma_start(out=xb[0][:, 1:4, :], in_=x_rows[0][:, 1:4, :])
        load_words(0, 0)
        load_wscales(0, nc.sync)
        nc.sync.dma_start(out=dec_bf[:], in_=dec.rearrange("b (g p t) h -> (b g) p (t h)", p=P, t=4).rearrange("n p c -> p n c"))
        nc.sync.dma_start(out=xb[1][:], in_=x_rows[1])
        load_wscales(1, nc.sync)
        nc.sync.dma_start(out=beta_bf[:], in_=beta.rearrange("b (g p t) -> (b g) p t", p=P, t=4).rearrange("n p t -> p n t"))
        load_words(1, 0)
        load_words(0, 1)
        load_words(1, 1)
        for n in range(2, N_GROUPS):
            nc.sync.dma_start(out=xb[n][:], in_=x_rows[n])
        nc.sync.dma_start(out=gamma_bf[:], in_=gamma.rearrange("b h -> (b h)").partition_broadcast(P))
        for b in range(B):
            nc.sync.dma_start(out=sp[b][:], in_=s_prev[b].rearrange("h (i p) j -> p (h i) j", p=P))

        xw, xin, planes, grouped = {}, {}, {}, {}

        def widen(n, t, blocks=range(J), on_scalar=False):
            if (n, t) not in xw:
                xw[n, t] = work.tile([P, D], BF16, name="xw", tag="xw", bufs=16, align_bytes=64)
            for j in blocks:
                dst = xw[n, t][:, 128 * j : 128 * (j + 1)]
                src = xb[n][:, t, 128 * j : 128 * (j + 1)].bitcast(E4M3FN)
                scale = xs[:, n, j : j + 1]
                if on_scalar:
                    nc.scalar.activation(out=dst, in_=src, func=COPY, scale=scale)
                else:
                    nc.vector.tensor_scalar(out=dst, in0=src, scalar1=scale, scalar2=None, op0=MULT)

        def turn(n, t):
            if t % 2 == 0:
                xin[n, t // 2] = work.tile([P, 2, G, P, 4], BF16, name="xin", tag="xin", bufs=4, align_bytes=64)
            bank = ring.tile([P, 512], F32, name="bank", tag="bank", bufs=6)
            view = bank[:].rearrange("p (g u m) -> p g u m", g=G, u=2)
            src = xw[n, t][:].bitcast(F32)
            for g in range(G):
                for u in range(2):
                    nc.tensor.transpose(view[:, g, u, :], src[:, 256 * g + u : 256 * (g + 1) : 2], ident[:])
            dst = xin[n, t // 2][:, t % 2].bitcast(F32)
            nc.scalar.copy(out=dst, in_=view.rearrange("p g u m -> p g m u"))

        def quant_x(n, t, count):
            cols = slice(256 * t, 256 * (t + count))
            src = xin[n, t // 2][:, t % 2 : t % 2 + count].rearrange("p t g m w -> p (t g m w)")
            nc.vector.quantize_mx(out=xq[n][:, cols].bitcast(E4M3X4), scales=xqs[n][:, cols], in_=src)

        def project(n, c, t):
            i, pair = c % 2, c // 2
            if t == 0:
                planes[n, c] = work.tile([P, 4, 512], BF16, name="planes", tag="planes", bufs=7, align_bytes=64)
            bank = ring.tile([P, 512], F32, name="bank", tag="bank", bufs=6)
            for g in range(G):
                rows = slice(256 * t + 128 * g, 256 * t + 128 * (g + 1))
                nc.tensor.matmul_mx(
                    out=bank[:],
                    lhsT=xq[n][:, rows].bitcast(E4M3X4),
                    lhsT_scale=xqs[n][:, rows],
                    rhs=words[i][:, g, 1024 * pair : 1024 * (pair + 1)].bitcast(E2M1X4),
                    rhs_scale=wsc[i][:, g, 512 * pair : 512 * (pair + 1)],
                    start=(g == 0),
                    stop=(g == G - 1),
                )
            dst = planes[n, c]
            if i == 0:
                for e in range(2):
                    col = 4 * t + 2 * pair + e
                    half = slice(256 * e, 256 * (e + 1))
                    nc.scalar.activation(out=dst[:, t, half], in_=bank[:, half], func=COPY, scale=dec32[:, n, col : col + 1])
            else:
                nc.scalar.activation(out=dst[:, t, :], in_=bank[:], func=COPY, scale=beta_f[:, n, t : t + 1])

        def interleave(n, c, first=0, last=512, copy=nc.vector.tensor_copy):
            if (n, c) not in grouped:
                grouped[n, c] = work.tile([P, 2048], BF16, name="grouped", tag="grouped", bufs=4, align_bytes=64)
            copy(
                out=grouped[n, c][:, 4 * first : 4 * last].rearrange("p (c i t) -> p c t i", i=4, t=4),
                in_=planes[n, c][:, :, first:last].rearrange("p t (c i) -> p c t i", i=4),
            )

        def quant(n, c, first=0, last=512):
            nc.vector.quantize_mx(
                out=kvq[n][c][:, first:last].bitcast(E4M3X4),
                scales=kvs[n][c][:, first:last],
                in_=grouped[n, c][:, 4 * first : 4 * last],
            )

        mixed = {}

        def mix(b, h):
            ck, off = 2 * (h // 2), 256 * (h % 2)
            bank = mixp.tile([P, 512], F32, name="mixbank", tag="mixbank", bufs=2)
            mixed[b, h] = bank
            for i in range(2):
                rows = slice(off + 128 * i, off + 128 * (i + 1))
                for g in range(2):
                    n = 2 * b + g
                    nc.tensor.matmul_mx(
                        out=bank[:, 256 * i : 256 * (i + 1)],
                        lhsT=kvq[n][ck][:, rows].bitcast(E4M3X4),
                        lhsT_scale=kvs[n][ck][:, rows],
                        rhs=kvq[n][ck + 1][:, off : off + 256].bitcast(E4M3X4),
                        rhs_scale=kvs[n][ck + 1][:, off : off + 256],
                        start=(g == 0),
                        stop=(g == 1),
                    )

        def finish(b, h, parts=1):
            res = work.tile([P, 512], F32, name="res", tag="res", bufs=4)
            state = sp[b][:, 2 * h : 2 * h + 2, :].rearrange("p i j -> p (i j)")
            width = 512 // parts
            for i in range(parts):
                cols = slice(width * i, width * (i + 1))
                nc.vector.scalar_tensor_tensor(
                    out=res[:, cols],
                    in0=state[:, cols],
                    scalar=gamma_bf[:, H * b + h : H * b + h + 1],
                    in1=mixed[b, h][:, cols],
                    op0=MULT,
                    op1=ADD,
                )
                rows = out[b, h].rearrange("(i p) j -> p i j", p=P)
                each = 2 // parts
                nc.sync.dma_start(out=rows[:, each * i : each * (i + 1), :], in_=res[:, cols].rearrange("p (i j) -> p i j", j=K))

        def project_all(n, c):
            for t in range(4):
                project(n, c, t)

        widen(0, 0)
        widen(0, 1)
        widen(0, 2)
        widen(0, 3, range(4), on_scalar=True)
        turn(0, 0)
        quant_x(0, 0, 1)
        widen(0, 3, range(4, J))
        turn(0, 1)
        quant_x(0, 1, 1)
        widen(1, 0)
        turn(0, 2)
        quant_x(0, 2, 1)
        widen(1, 1)
        turn(0, 3)
        quant_x(0, 3, 1)
        for n, t in ((1, 2), (1, 3), (2, 0), (2, 1)):
            widen(n, t)
        nc.scalar.activation(out=dec32[:], in_=dec_bf[:], func=COPY, scale=1.0 / 32.0)

        fill = {}
        fill[0, 2] = [(widen, (2, 2)), (widen, (2, 3))]
        fill[0, 3] = [(widen, (3, 0)), (widen, (3, 1))]
        fill[1, 2] = [(widen, (3, 2))]
        fill[1, 3] = [(widen, (3, 3))]
        fill[2, 2] = [(finish, (0, 0)), (finish, (0, 1))]
        fill[3, 0] = [(finish, (0, 2)), (finish, (0, 3))]
        for n in range(N_GROUPS - 1):
            fill[n, 1] = [(quant_x, (n + 1, 0, 2)), (quant_x, (n + 1, 2, 2))]
        heads = {(2, 2): (0, 0), (3, 0): (0, 2), (3, 3): (1, 0)}

        for n in range(N_GROUPS):
            for c in range(4):
                if (n, c) == (0, 1):
                    nc.scalar.copy(out=beta_f[:], in_=beta_bf[:])
                project_all(n, c)
                if n + 1 < N_GROUPS and c == 1:
                    for t in range(4):
                        turn(n + 1, t)
                if (n, c) in heads:
                    b, h = heads[n, c]
                    mix(b, h)
                    mix(b, h + 1)
                if (n, c) == (3, 3):
                    finish(1, 0)
                    finish(1, 1)
                    interleave(n, c, 0, 256)
                    interleave(n, c, 384, 512, nc.scalar.copy)
                    interleave(n, c, 256, 384)
                    quant(n, c, 0, 256)
                    quant(n, c, 256, 512)
                elif (n, c) in fill:
                    interleave(n, c)
                    for step, args in fill[n, c]:
                        step(*args)
                    quant(n, c)
                else:
                    interleave(n, c, 0, 256)
                    interleave(n, c, 256, 512)
                    quant(n, c, 0, 256)
                    quant(n, c, 256, 512)
        mix(1, 2)
        mix(1, 3)
        finish(1, 2)
        finish(1, 3, 2)
